import numpy as np
import ml_dtypes


def mxq(x, axis, fmt="e4m3"):
    dtype, down = {"e4m3": (ml_dtypes.float8_e4m3fn, 7), "e5m2": (ml_dtypes.float8_e5m2, 14)}[fmt]
    v = np.moveaxis(np.asarray(x, np.float32).astype(ml_dtypes.bfloat16).astype(np.float64), axis, -1)
    blocks = v.reshape(v.shape[:-1] + (-1, 32))
    amax = np.abs(blocks).max(-1, keepdims=True)
    byte = np.maximum(np.where(amax > 0, np.frexp(amax)[1] - 1 + 127, 0) - down, 1)
    scale = np.exp2(byte - 127.0)
    codes = (blocks / scale).astype(np.float32).astype(dtype).astype(np.float64)
    return np.moveaxis((codes * scale).reshape(v.shape), -1, axis)


WIDE = False


def mx_kscale(k):
    if not WIDE:
        return np.ones(k)
    levels = np.array([10, -10, 5, -5, 0])
    if k % 512:
        return np.exp2(np.random.permutation(np.resize(levels, k // 32))).repeat(32)
    a = np.empty((k // 512, 16))
    for p in range(k // 512):
        a[p, :8] = np.random.permutation(np.resize(levels, 8))
        for g in range(8):
            far = levels[np.abs(levels - a[p, g]) >= 10]
            a[p, g + 8] = far[np.random.randint(len(far))]
    return np.exp2(a.ravel()).repeat(32)


def f64(x):
    return np.asarray(x).astype(np.float64)


def striped(idx):
    return np.tile(np.asarray(idx).reshape(-1, 16).T, (8, 1)).astype(np.uint16)


def unstriped(offs):
    return offs[:16].T.reshape(-1).astype(np.int64)


E2M1 = np.array([0.0, 0.5, 1.0, 1.5, 2.0, 3.0, 4.0, 6.0, -0.0, -0.5, -1.0, -1.5, -2.0, -3.0, -4.0, -6.0])


def pack_weight(w, fmt):
    k, n = w.shape
    w = f64(np.asarray(w, np.float32).astype(ml_dtypes.bfloat16)).reshape(k // 32, 32, n)
    amax = np.abs(w).max(1)
    if fmt == "e4m3":
        byte = np.frexp(amax)[1] - 1 + 127 - 7
    else:
        mant, ex = np.frexp(amax / 6.0)
        byte = np.where(mant > 0.5, ex, ex - 1) + 127
    byte = np.clip(np.where(amax > 0, byte, 1), 1, 254)
    scaled = (w * np.exp2(127.0 - byte)[:, None, :]).reshape(k, n).astype(np.float32)
    by_word = np.ascontiguousarray(scaled.reshape(k // 512, 128, 4, n).transpose(0, 1, 3, 2))
    if fmt == "e4m3":
        words = by_word.astype(ml_dtypes.float8_e4m3fn).view(np.uint8)
    else:
        c = by_word.astype(ml_dtypes.float4_e2m1fn).view(np.uint8) & 0xF
        words = (c[..., 0::2] | (c[..., 1::2] << 4)).reshape(k // 512, 128, 2 * n)
    return np.ascontiguousarray(words), np.ascontiguousarray(byte.astype(np.uint8).reshape(k // 512, 16, n))


def unpack_weight(words, scales, fmt):
    g, _, n = scales.shape
    words = np.ascontiguousarray(words).reshape(g, 128, n, -1)
    if fmt == "e4m3":
        vals = words.view(ml_dtypes.float8_e4m3fn).astype(np.float64)
    else:
        nib = np.empty((g, 128, n, 4), np.uint8)
        nib[..., 0::2] = words & 0xF
        nib[..., 1::2] = words >> 4
        vals = E2M1[nib]
    vals = vals * np.repeat(np.exp2(scales.astype(np.float64) - 127.0), 8, axis=1)[..., None]
    return vals.transpose(0, 1, 3, 2).reshape(g * 512, n)


D, E, T, I, Q = 512, 512, 2048, 512, 128


def setup_inputs():
    n = np.random.standard_normal
    idx = np.random.permutation(T)[:I]
    fd = mx_kscale(D)
    fe = mx_kscale(E)
    keysp = pack_weight(n((D, T)) / fd[:, None], "e2m1")
    valsp = pack_weight(n((E, T)) / fe[:, None], "e2m1")
    return {
        "query": (n((D, Q)) * 0.9 / np.sqrt(D) * fd[:, None]).astype(np.float32),
        "query2": (n((D, Q)) * 0.6 / np.sqrt(D) * fd[:, None]).astype(np.float32),
        "keys_words": keysp[0],
        "keys_scales": keysp[1],
        "gout": (n((E, Q)) * 1 / np.sqrt(E) * fe[:, None]).astype(np.float32),
        "vals_words": valsp[0],
        "vals_scales": valsp[1],
        "size": (np.random.uniform(0.5, 2.0, (1, I))).astype(np.float32),
        "base": (0.5 * n((Q, T))).astype(np.float32),
        "gq1": (np.random.uniform(0.3, 1.5, (Q, 1))).astype(np.float32),
        "offs": striped(idx),
    }


def reference(query, query2, keys_words, keys_scales, gout, vals_words, vals_scales, size, base, gq1, offs):
    idx = unstriped(offs)
    keysu = unpack_weight(keys_words, keys_scales, "e2m1")
    valsu = unpack_weight(vals_words, vals_scales, "e2m1")
    queryq = mxq(f64(query), 0, "e4m3")
    keysidxg = keysu[:, idx]
    a = queryq.T @ keysidxg
    query2q = mxq(f64(query2), 0, "e4m3")
    b = query2q.T @ keysidxg
    pa = np.exp(a - np.max(a, axis=1, keepdims=True))
    wa = pa / np.sum(pa, axis=1, keepdims=True)
    pb = np.exp(b - np.max(b, axis=1, keepdims=True))
    wb = pb / np.sum(pb, axis=1, keepdims=True)
    goutq = mxq(f64(gout), 0, "e4m3")
    valsidxg = valsu[:, idx]
    c0 = goutq.T @ valsidxg
    dwa = c0 * f64(size) / (wa + wb) * wb - c0 * f64(size) * wa * wb / np.square(wa + wb)
    dpa = dwa / np.sum(pa, axis=1, keepdims=True) + np.sum(dwa * pa / np.square(np.sum(pa, axis=1, keepdims=True)) * (-1.0), axis=1, keepdims=True)
    da = dpa * pa
    hda = da * 512.0 * 2.0 * 512.0
    hdpa = hda * pa
    hdwa = hdpa / np.sum(pa, axis=1, keepdims=True) + np.sum(hdpa, axis=1, keepdims=True) * (-1.0) / np.square(np.sum(pa, axis=1, keepdims=True)) * pa
    hwa = hdwa * (-1.0) / np.square(wa + wb) * c0 * f64(size) * wb + hdwa * (-1.0) * c0 * f64(size) * wa * wb / np.square(np.square(wa + wb)) * (-1.0) * (wa + wb) * 2.0 - hdwa * wb * c0 * f64(size) / np.square(wa + wb)
    hpa = hda * dpa + np.sum(hdpa * dwa / np.square(np.sum(pa, axis=1, keepdims=True)) * (-1.0), axis=1, keepdims=True) + np.sum(hdpa, axis=1, keepdims=True) * (-1.0) / np.square(np.sum(pa, axis=1, keepdims=True)) * dwa + np.sum(np.sum(hdpa, axis=1, keepdims=True) * (-1.0) * dwa * pa / np.square(np.square(np.sum(pa, axis=1, keepdims=True))) * (-1.0), axis=1, keepdims=True) * np.sum(pa, axis=1, keepdims=True) * 2.0 + hwa / np.sum(pa, axis=1, keepdims=True) + np.sum(hwa * pa / np.square(np.sum(pa, axis=1, keepdims=True)) * (-1.0), axis=1, keepdims=True)
    ha = hpa * pa
    gs = ha * f64(gq1)
    gf = np.zeros((Q, T))
    gf[:, idx] = gs
    y = f64(base) + gf
    return y

@@ -1,0 +1,203 @@
+import math
+from contextlib import ExitStack
+
+import concourse.mybir as mybir
+from concourse.masks import make_identity
+
+D, E, T, I, Q = 512, 512, 2048, 512, 128
+FLOPS = 3 * 2 * D * Q * I
+
+F32 = mybir.dt.float32
+BF16 = mybir.dt.bfloat16
+I32 = mybir.dt.int32
+U32 = mybir.dt.uint32
+U16 = mybir.dt.uint16
+U8 = mybir.dt.uint8
+FP8X4 = mybir.dt.float8_e4m3fn_x4
+FP4X4 = mybir.dt.float4_e2m1fn_x4
+ALU = mybir.AluOpType
+ACT = mybir.ActivationFunctionType
+AX = mybir.AxisListType
+
+P = 128
+PACK = 4
+TERMS = 20
+EXPONENT_BITS = 0x7F800000
+PENALTY = 512.0 * 2.0 * 512.0
+STORE_COLS = 512
+
+
+def tile_attend_gpagreement_kernel(tc, query, query2, keys_words, keys_scales, gout, vals_words, vals_scales, size, base, gq1, offs, out):
+    nc = tc.nc
+    with ExitStack() as ctx:
+        sb = ctx.enter_context(tc.tile_pool(name="sb", bufs=1))
+        ps = ctx.enter_context(tc.psum_pool(name="ps", bufs=1))
+
+        def tile(name, cols, dtype=F32, tag=None):
+            return sb.tile([P, cols], dtype, name=name, tag=tag or name, align_bytes=64)
+
+        offsets = sb.tile([P, I // 16], U16, name="offsets")
+        k_words = tile("k_words", T, U16)
+        k_scales = tile("k_scales", T, U8)
+        v_scales = tile("v_scales", T, U8)
+        window = tile("window", T)
+
+        nc.vector.memset(k_scales[:].bitcast(I32), 0)
+        nc.vector.memset(v_scales[:].bitcast(I32), 0)
+
+        def load_scales(dst, src):
+            for quad in range(4):
+                nc.sync.dma_start(dst[32 * quad : 32 * quad + 4, :].bitcast(I32), src[0, 4 * quad : 4 * quad + 4, :].bitcast(I32))
+
+        def load_rows(name, src, tag=None):
+            raw = sb.tile([P, PACK, Q], F32, name=name, tag=tag or name, align_bytes=64)
+            nc.sync.dma_start(raw[:], src.rearrange("(p j) w -> p j w", j=PACK))
+            return raw
+
+        nc.sync.dma_start(offsets[:], offs)
+        nc.sync.dma_start(k_words[:].bitcast(I32), keys_words[0].bitcast(I32))
+        load_scales(k_scales, keys_scales)
+        q1_raw = load_rows("q1_raw", query)
+        q2_raw = load_rows("q2_raw", query2)
+        load_scales(v_scales, vals_scales)
+        go_raw = load_rows("go_raw", gout)
+        v_words = tile("v_words", T, U16)
+        nc.sync.dma_start(v_words[:].bitcast(I32), vals_words[0].bitcast(I32))
+        base_sb = tile("base_sb", T)
+        nc.sync.dma_start(base_sb[:], base)
+
+        order = tile("order", TERMS)
+        nc.gpsimd.iota(order[:], pattern=[[-1, TERMS]], base=TERMS, channel_multiplier=0, allow_small_or_imprecise_dtypes=True)
+        size_col = tile("size_col", PACK)
+        nc.gpsimd.dma_start(size_col[:], size.rearrange("o (p j) -> (o p) j", j=PACK))
+        row_factor = tile("row_factor", 1)
+        nc.gpsimd.dma_start(row_factor[:], gq1)
+        ident = tile("ident", P)
+        make_identity(nc, ident[:])
+
+        powers = tile("powers", TERMS)
+        nc.scalar.activation(powers[:], order[:], ACT.Exp, scale=-math.log(3.0))
+        inv_order = tile("inv_order", TERMS)
+        nc.vector.reciprocal(inv_order[:], order[:])
+        series = tile("series", TERMS + 2)
+        nc.vector.scalar_tensor_tensor(series[:, :TERMS], powers[:], 0.5, inv_order[:], ALU.mult, ALU.mult)
+        ws = tile("ws", I)
+        horner_x = ws[:, : TERMS + 2]
+        nc.vector.memset(horner_x[:, TERMS + 1 :], 1.0)
+        nc.vector.memset(window[:], 0.0)
+
+        def interleave(name, raw):
+            grouped = sb.tile([P, Q, PACK], BF16, name=name, align_bytes=64)
+            nc.scalar.copy(grouped[:], raw[:].rearrange("p j w -> p w j"))
+            return grouped
+
+        def quantize(name, grouped, tag=None):
+            codes = tile(name + "_codes", Q, U32, tag=tag)
+            scales = tile(name + "_scales", Q, U8)
+            nc.vector.quantize_mx(codes[:].bitcast(FP8X4), scales[:], grouped[:].rearrange("p w j -> p (w j)"))
+            return codes, scales
+
+        def gather(name, pool_tile, dtype, tag=None):
+            picked = tile(name, I, dtype, tag=tag)
+            nc.vector.tensor_copy(picked[:], pool_tile[:].indirect(offsets[:]))
+            return picked
+
+        def product(name, rows, words, scales):
+            acc = ps.tile([P, I], F32, name=name)
+            nc.tensor.matmul_mx(acc[:], lhsT=rows[0][:].bitcast(FP8X4), lhsT_scale=rows[1][:], rhs=words[:].bitcast(FP4X4), rhs_scale=scales[:], start=True, stop=True)
+            return acc
+
+        q1_bf = interleave("q1_bf", q1_raw)
+        q2_bf = interleave("q2_bf", q2_raw)
+        go_bf = interleave("go_bf", go_raw)
+
+        kg_words = gather("kg_words", k_words, U16)
+        kg_scales = gather("kg_scales", k_scales, U8)
+        q1_mx = quantize("q1", q1_bf)
+        a_ps = product("a_ps", q1_mx, kg_words, kg_scales)
+        q2_mx = quantize("q2", q2_bf)
+        b_ps = product("b_ps", q2_mx, kg_words, kg_scales)
+        vg_scales = gather("vg_scales", v_scales, U8)
+
+        size_ps = ps.tile([P, PACK, P], F32, name="size_ps")
+        for j in range(PACK):
+            nc.tensor.transpose(size_ps[:, j, :], size_col[:, j : j + 1].to_broadcast([P, P]), ident[:])
+
+        neg_a = tile("neg_a", I, tag="v_scales")
+        neg_max_a = tile("neg_max_a", 1)
+        nc.vector.tensor_scalar(neg_a[:], a_ps[:], -1.0, None, ALU.mult, ALU.min, accum_out=neg_max_a[:])
+        neg_max_b = tile("neg_max_b", 1)
+        nc.vector.tensor_reduce(neg_max_b[:], b_ps[:], AX.X, ALU.max, negate=True)
+
+        pa = tile("pa", I, tag="go_raw")
+        sum_a = tile("sum_a", 1)
+        nc.scalar.activation(pa[:], a_ps[:], ACT.Exp, bias=neg_max_a[:], accum_out=sum_a[:])
+        pb = tile("pb", I)
+        sum_b = tile("sum_b", 1)
+        nc.scalar.activation(pb[:], b_ps[:], ACT.Exp, bias=neg_max_b[:], accum_out=sum_b[:])
+
+        inv_sum_a = tile("inv_sum_a", 1)
+        nc.vector.reciprocal(inv_sum_a[:], sum_a[:])
+        nc.vector.tensor_scalar(series[:, TERMS + 1 :], neg_max_b[:], neg_max_a[:], 0.5, ALU.subtract, ALU.mult)
+        wa = tile("wa", I)
+        nc.scalar.activation(wa[:], pa[:], ACT.Copy, scale=inv_sum_a[:])
+
+        go_mx = quantize("go", go_bf, tag="q2_codes")
+        vg_words = gather("vg_words", v_words, U16, tag="go_bf")
+        c_ps = product("c_ps", go_mx, vg_words, vg_scales)
+
+        neg_ratio = tile("neg_ratio", 1, tag="v_words")
+        nc.vector.tensor_scalar(neg_ratio[:], sum_b[:], inv_sum_a[:], -1.0, ALU.mult, ALU.mult)
+        pow2 = tile("pow2", 1, I32)
+        nc.vector.tensor_scalar(pow2[:], neg_ratio[:].bitcast(I32), EXPONENT_BITS, EXPONENT_BITS, ALU.bitwise_and, ALU.bitwise_xor)
+        nc.vector.tensor_scalar(horner_x[:, : TERMS + 1], neg_ratio[:].to_broadcast([P, TERMS + 1]), pow2[:].bitcast(F32), 3.0, ALU.mult, ALU.add)
+        nc.vector.tensor_scalar(series[:, TERMS : TERMS + 1], pow2[:], 0.5 * math.log(2.0) / 2.0**23, -0.5 * (math.log(3.0) + 127.0 * math.log(2.0)), ALU.mult, ALU.add)
+        horner = tile("horner", TERMS + 2)
+        nc.vector.tensor_tensor_scan(horner[:], horner_x, series[:], 0.0, ALU.mult, ALU.add)
+
+        diff = tile("diff", I, tag="sum_b")
+        for half in (slice(0, I // 2), slice(I // 2, I)):
+            nc.vector.tensor_tensor(diff[:, half], b_ps[:, half], neg_a[:, half], ALU.add)
+        y = tile("y", I)
+        nc.scalar.activation(y[:], diff[:], ACT.Tanh, bias=horner[:, TERMS + 1 :], scale=0.5)
+        r2 = tile("r2", I)
+        nc.scalar.activation(r2[:], y[:], ACT.Square, bias=0.5, scale=0.5)
+
+        factor = tile("factor", 1)
+        nc.vector.tensor_scalar_mul(factor[:], row_factor[:], PENALTY)
+        wac = tile("wac", I)
+        nc.scalar.activation(wac[:], wa[:], ACT.Copy, scale=factor[:])
+
+        nc.vector.tensor_tensor(
+            ws[:].rearrange("p (s j) -> p s j", j=PACK),
+            size_ps[:].rearrange("p j s -> p s j"),
+            wa[:].rearrange("p (s j) -> p s j", j=PACK),
+            ALU.mult,
+        )
+        wv = tile("wv", I)
+        nc.vector.tensor_tensor(wv[:], c_ps[:], ws[:], ALU.mult)
+
+        wd = tile("wd", I)
+        m = tile("m", 1)
+        nc.vector.scalar_tensor_tensor(wd[:], r2[:], 1.0, wv[:], ALU.mult, ALU.mult, accum_out=m[:])
+        wdy = tile("wdy", I)
+        nc.vector.scalar_tensor_tensor(wdy[:], y[:], factor[:], wd[:], ALU.mult, ALU.mult)
+        neg_da = tile("neg_da", I)
+        nc.vector.scalar_tensor_tensor(neg_da[:], wa[:], m[:], wd[:], ALU.mult, ALU.subtract)
+        neg_wz = tile("neg_wz", I)
+        nc.vector.scalar_tensor_tensor(neg_wz[:], wac[:], m[:], wdy[:], ALU.mult, ALU.subtract)
+        neg_n = tile("neg_n", 1)
+        wada = tile("wada", I)
+        nc.vector.scalar_tensor_tensor(wada[:], neg_da[:], 1.0, wa[:], ALU.mult, ALU.mult, accum_out=neg_n[:])
+        wt = tile("wt", I)
+        total = tile("total", 1)
+        nc.vector.scalar_tensor_tensor(wt[:], neg_da[:], neg_n[:], neg_wz[:], ALU.subtract, ALU.mult, accum_out=total[:])
+        tw = tile("tw", I)
+        nc.vector.tensor_scalar(tw[:], wa[:], total[:], -1.0, ALU.mult, ALU.mult)
+        nc.vector.tensor_tensor(window[:].indirect(offsets[:]), wt[:], tw[:], ALU.add)
+
+        for n, c0 in enumerate(range(0, T, STORE_COLS)):
+            cols = slice(c0, c0 + STORE_COLS)
+            nc.vector.tensor_tensor(base_sb[:, cols], base_sb[:, cols], window[:, cols], ALU.add)
+            queue = nc.sync if n % 2 == 0 else nc.scalar
+            queue.dma_start(out[:, cols], base_sb[:, cols])

@@ -24,7 +24,7 @@ PACK = 4
 TERMS = 20
 EXPONENT_BITS = 0x7F800000
 PENALTY = 512.0 * 2.0 * 512.0
-STORE_COLS = 512
+STORE_EDGES = (0, 256, 768, 1280, 1792, 2048)
 
 
 def tile_attend_gpagreement_kernel(tc, query, query2, keys_words, keys_scales, gout, vals_words, vals_scales, size, base, gq1, offs, out):
@@ -37,17 +37,16 @@ def tile_attend_gpagreement_kernel(tc, query, query2, keys_words, keys_scales, g
             return sb.tile([P, cols], dtype, name=name, tag=tag or name, align_bytes=64)
 
         offsets = sb.tile([P, I // 16], U16, name="offsets")
-        k_words = tile("k_words", T, U16)
         k_scales = tile("k_scales", T, U8)
         v_scales = tile("v_scales", T, U8)
         window = tile("window", T)
 
-        nc.vector.memset(k_scales[:].bitcast(I32), 0)
-        nc.vector.memset(v_scales[:].bitcast(I32), 0)
+        nc.gpsimd.memset(k_scales[:].bitcast(I32), 0)
+        nc.gpsimd.memset(v_scales[:].bitcast(I32), 0)
 
         def load_scales(dst, src):
-            for quad in range(4):
-                nc.sync.dma_start(dst[32 * quad : 32 * quad + 4, :].bitcast(I32), src[0, 4 * quad : 4 * quad + 4, :].bitcast(I32))
+            for r in range(4):
+                nc.sync.dma_start(dst[r:P:32, :].bitcast(I32), src[0, r:16:4, :].bitcast(I32))
 
         def load_rows(name, src, tag=None):
             raw = sb.tile([P, PACK, Q], F32, name=name, tag=tag or name, align_bytes=64)
@@ -55,23 +54,24 @@ def tile_attend_gpagreement_kernel(tc, query, query2, keys_words, keys_scales, g
             return raw
 
         nc.sync.dma_start(offsets[:], offs)
-        nc.sync.dma_start(k_words[:].bitcast(I32), keys_words[0].bitcast(I32))
+        row_factor = tile("row_factor", 1)
+        nc.sync.dma_start(row_factor[:], gq1)
         load_scales(k_scales, keys_scales)
+        k_words = tile("k_words", T, U16)
+        nc.sync.dma_start(k_words[:].bitcast(I32), keys_words[0].bitcast(I32))
         q1_raw = load_rows("q1_raw", query)
-        q2_raw = load_rows("q2_raw", query2)
         load_scales(v_scales, vals_scales)
+        q2_raw = load_rows("q2_raw", query2)
         go_raw = load_rows("go_raw", gout)
         v_words = tile("v_words", T, U16)
         nc.sync.dma_start(v_words[:].bitcast(I32), vals_words[0].bitcast(I32))
+        size_col = tile("size_col", PACK)
+        nc.sync.dma_start(size_col[:], size.rearrange("o (p j) -> (o p) j", j=PACK))
         base_sb = tile("base_sb", T)
         nc.sync.dma_start(base_sb[:], base)
 
         order = tile("order", TERMS)
         nc.gpsimd.iota(order[:], pattern=[[-1, TERMS]], base=TERMS, channel_multiplier=0, allow_small_or_imprecise_dtypes=True)
-        size_col = tile("size_col", PACK)
-        nc.gpsimd.dma_start(size_col[:], size.rearrange("o (p j) -> (o p) j", j=PACK))
-        row_factor = tile("row_factor", 1)
-        nc.gpsimd.dma_start(row_factor[:], gq1)
         ident = tile("ident", P)
         make_identity(nc, ident[:])
 
@@ -111,19 +111,19 @@ def tile_attend_gpagreement_kernel(tc, query, query2, keys_words, keys_scales, g
         q2_bf = interleave("q2_bf", q2_raw)
         go_bf = interleave("go_bf", go_raw)
 
-        kg_words = gather("kg_words", k_words, U16)
         kg_scales = gather("kg_scales", k_scales, U8)
+        kg_words = gather("kg_words", k_words, U16)
         q1_mx = quantize("q1", q1_bf)
         a_ps = product("a_ps", q1_mx, kg_words, kg_scales)
+        vg_scales = gather("vg_scales", v_scales, U8, tag="q1_bf")
         q2_mx = quantize("q2", q2_bf)
         b_ps = product("b_ps", q2_mx, kg_words, kg_scales)
-        vg_scales = gather("vg_scales", v_scales, U8)
 
         size_ps = ps.tile([P, PACK, P], F32, name="size_ps")
         for j in range(PACK):
             nc.tensor.transpose(size_ps[:, j, :], size_col[:, j : j + 1].to_broadcast([P, P]), ident[:])
 
-        neg_a = tile("neg_a", I, tag="v_scales")
+        neg_a = tile("neg_a", I, tag="q2_bf")
         neg_max_a = tile("neg_max_a", 1)
         nc.vector.tensor_scalar(neg_a[:], a_ps[:], -1.0, None, ALU.mult, ALU.min, accum_out=neg_max_a[:])
         neg_max_b = tile("neg_max_b", 1)
@@ -143,10 +143,17 @@ def tile_attend_gpagreement_kernel(tc, query, query2, keys_words, keys_scales, g
         nc.scalar.activation(wa[:], pa[:], ACT.Copy, scale=inv_sum_a[:])
 
         go_mx = quantize("go", go_bf, tag="q2_codes")
-        vg_words = gather("vg_words", v_words, U16, tag="go_bf")
-        c_ps = product("c_ps", go_mx, vg_words, vg_scales)
+        c_ps = ps.tile([P, I], F32, name="c_ps")
 
-        neg_ratio = tile("neg_ratio", 1, tag="v_words")
+        def values_half(h, tag):
+            picked = tile("vg_words%d" % h, I // 2, U16, tag=tag)
+            nc.vector.tensor_copy(picked[:], v_words[:].indirect(offsets[:, h * I // 32 : (h + 1) * I // 32]))
+            cols = slice(h * I // 2, (h + 1) * I // 2)
+            nc.tensor.matmul_mx(c_ps[:, cols], lhsT=go_mx[0][:].bitcast(FP8X4), lhsT_scale=go_mx[1][:], rhs=picked[:].bitcast(FP4X4), rhs_scale=vg_scales[:, cols], start=True, stop=True)
+
+        values_half(0, "go_bf")
+
+        neg_ratio = tile("neg_ratio", 1)
         nc.vector.tensor_scalar(neg_ratio[:], sum_b[:], inv_sum_a[:], -1.0, ALU.mult, ALU.mult)
         pow2 = tile("pow2", 1, I32)
         nc.vector.tensor_scalar(pow2[:], neg_ratio[:].bitcast(I32), EXPONENT_BITS, EXPONENT_BITS, ALU.bitwise_and, ALU.bitwise_xor)
@@ -155,7 +162,8 @@ def tile_attend_gpagreement_kernel(tc, query, query2, keys_words, keys_scales, g
         horner = tile("horner", TERMS + 2)
         nc.vector.tensor_tensor_scan(horner[:], horner_x, series[:], 0.0, ALU.mult, ALU.add)
 
-        diff = tile("diff", I, tag="sum_b")
+        values_half(1, "sum_b")
+        diff = tile("diff", I, tag="pb")
         for half in (slice(0, I // 2), slice(I // 2, I)):
             nc.vector.tensor_tensor(diff[:, half], b_ps[:, half], neg_a[:, half], ALU.add)
         y = tile("y", I)
@@ -196,8 +204,8 @@ def tile_attend_gpagreement_kernel(tc, query, query2, keys_words, keys_scales, g
         nc.vector.tensor_scalar(tw[:], wa[:], total[:], -1.0, ALU.mult, ALU.mult)
         nc.vector.tensor_tensor(window[:].indirect(offsets[:]), wt[:], tw[:], ALU.add)
 
-        for n, c0 in enumerate(range(0, T, STORE_COLS)):
-            cols = slice(c0, c0 + STORE_COLS)
+        for n in range(len(STORE_EDGES) - 1):
+            cols = slice(STORE_EDGES[n], STORE_EDGES[n + 1])
             nc.vector.tensor_tensor(base_sb[:, cols], base_sb[:, cols], window[:, cols], ALU.add)
             queue = nc.sync if n % 2 == 0 else nc.scalar
             queue.dma_start(out[:, cols], base_sb[:, cols])

@@ -17,7 +17,6 @@ FP8X4 = mybir.dt.float8_e4m3fn_x4
 FP4X4 = mybir.dt.float4_e2m1fn_x4
 ALU = mybir.AluOpType
 ACT = mybir.ActivationFunctionType
-AX = mybir.AxisListType
 
 P = 128
 PACK = 4
@@ -41,8 +40,8 @@ def tile_attend_gpagreement_kernel(tc, query, query2, keys_words, keys_scales, g
         v_scales = tile("v_scales", T, U8)
         window = tile("window", T)
 
-        nc.gpsimd.memset(k_scales[:].bitcast(I32), 0)
-        nc.gpsimd.memset(v_scales[:].bitcast(I32), 0)
+        nc.vector.memset(k_scales[:].bitcast(I32), 0)
+        nc.vector.memset(v_scales[:].bitcast(I32), 0)
 
         def load_scales(dst, src):
             for r in range(4):
@@ -54,19 +53,19 @@ def tile_attend_gpagreement_kernel(tc, query, query2, keys_words, keys_scales, g
             return raw
 
         nc.sync.dma_start(offsets[:], offs)
-        row_factor = tile("row_factor", 1)
-        nc.sync.dma_start(row_factor[:], gq1)
-        load_scales(k_scales, keys_scales)
         k_words = tile("k_words", T, U16)
         nc.sync.dma_start(k_words[:].bitcast(I32), keys_words[0].bitcast(I32))
+        load_scales(k_scales, keys_scales)
         q1_raw = load_rows("q1_raw", query)
-        load_scales(v_scales, vals_scales)
         q2_raw = load_rows("q2_raw", query2)
+        load_scales(v_scales, vals_scales)
         go_raw = load_rows("go_raw", gout)
         v_words = tile("v_words", T, U16)
         nc.sync.dma_start(v_words[:].bitcast(I32), vals_words[0].bitcast(I32))
         size_col = tile("size_col", PACK)
         nc.sync.dma_start(size_col[:], size.rearrange("o (p j) -> (o p) j", j=PACK))
+        row_factor = tile("row_factor", 1)
+        nc.sync.dma_start(row_factor[:], gq1)
         base_sb = tile("base_sb", T)
         nc.sync.dma_start(base_sb[:], base)
 
@@ -79,11 +78,15 @@ def tile_attend_gpagreement_kernel(tc, query, query2, keys_words, keys_scales, g
         nc.scalar.activation(powers[:], order[:], ACT.Exp, scale=-math.log(3.0))
         inv_order = tile("inv_order", TERMS)
         nc.vector.reciprocal(inv_order[:], order[:])
-        series = tile("series", TERMS + 2)
-        nc.vector.scalar_tensor_tensor(series[:, :TERMS], powers[:], 0.5, inv_order[:], ALU.mult, ALU.mult)
+        series = tile("series", TERMS + 4)
+        nc.vector.tensor_tensor(series[:, :TERMS], powers[:], inv_order[:], ALU.mult)
+        nc.vector.memset(series[:, TERMS + 3 :], 0.0)
+        neg_max_b = series[:, TERMS + 1 : TERMS + 2]
+        neg_max_a = series[:, TERMS + 2 : TERMS + 3]
         ws = tile("ws", I)
-        horner_x = ws[:, : TERMS + 2]
-        nc.vector.memset(horner_x[:, TERMS + 1 :], 1.0)
+        horner_x = ws[:, : TERMS + 4]
+        for col, value in ((TERMS + 1, 1.0), (TERMS + 2, -1.0), (TERMS + 3, -0.5)):
+            nc.vector.memset(horner_x[:, col : col + 1], value)
         nc.vector.memset(window[:], 0.0)
 
         def interleave(name, raw):
@@ -111,23 +114,23 @@ def tile_attend_gpagreement_kernel(tc, query, query2, keys_words, keys_scales, g
         q2_bf = interleave("q2_bf", q2_raw)
         go_bf = interleave("go_bf", go_raw)
 
-        kg_scales = gather("kg_scales", k_scales, U8)
         kg_words = gather("kg_words", k_words, U16)
+        kg_scales = gather("kg_scales", k_scales, U8)
         q1_mx = quantize("q1", q1_bf)
         a_ps = product("a_ps", q1_mx, kg_words, kg_scales)
-        vg_scales = gather("vg_scales", v_scales, U8, tag="q1_bf")
         q2_mx = quantize("q2", q2_bf)
         b_ps = product("b_ps", q2_mx, kg_words, kg_scales)
+        vg_scales = gather("vg_scales", v_scales, U8)
 
         size_ps = ps.tile([P, PACK, P], F32, name="size_ps")
         for j in range(PACK):
             nc.tensor.transpose(size_ps[:, j, :], size_col[:, j : j + 1].to_broadcast([P, P]), ident[:])
 
-        neg_a = tile("neg_a", I, tag="q2_bf")
-        neg_max_a = tile("neg_max_a", 1)
+        neg_scores = tile("neg_scores", 2 * I, tag="v_scales")
+        neg_a = neg_scores[:, :I]
+        neg_b = neg_scores[:, I:]
         nc.vector.tensor_scalar(neg_a[:], a_ps[:], -1.0, None, ALU.mult, ALU.min, accum_out=neg_max_a[:])
-        neg_max_b = tile("neg_max_b", 1)
-        nc.vector.tensor_reduce(neg_max_b[:], b_ps[:], AX.X, ALU.max, negate=True)
+        nc.vector.tensor_scalar(neg_b[:], b_ps[:], -1.0, None, ALU.mult, ALU.min, accum_out=neg_max_b[:])
 
         pa = tile("pa", I, tag="go_raw")
         sum_a = tile("sum_a", 1)
@@ -138,7 +141,6 @@ def tile_attend_gpagreement_kernel(tc, query, query2, keys_words, keys_scales, g
 
         inv_sum_a = tile("inv_sum_a", 1)
         nc.vector.reciprocal(inv_sum_a[:], sum_a[:])
-        nc.vector.tensor_scalar(series[:, TERMS + 1 :], neg_max_b[:], neg_max_a[:], 0.5, ALU.subtract, ALU.mult)
         wa = tile("wa", I)
         nc.scalar.activation(wa[:], pa[:], ACT.Copy, scale=inv_sum_a[:])
 
@@ -158,8 +160,8 @@ def tile_attend_gpagreement_kernel(tc, query, query2, keys_words, keys_scales, g
         pow2 = tile("pow2", 1, I32)
         nc.vector.tensor_scalar(pow2[:], neg_ratio[:].bitcast(I32), EXPONENT_BITS, EXPONENT_BITS, ALU.bitwise_and, ALU.bitwise_xor)
         nc.vector.tensor_scalar(horner_x[:, : TERMS + 1], neg_ratio[:].to_broadcast([P, TERMS + 1]), pow2[:].bitcast(F32), 3.0, ALU.mult, ALU.add)
-        nc.vector.tensor_scalar(series[:, TERMS : TERMS + 1], pow2[:], 0.5 * math.log(2.0) / 2.0**23, -0.5 * (math.log(3.0) + 127.0 * math.log(2.0)), ALU.mult, ALU.add)
-        horner = tile("horner", TERMS + 2)
+        nc.vector.tensor_scalar(series[:, TERMS : TERMS + 1], pow2[:], math.log(2.0) / 2.0**23, -(math.log(3.0) + 127.0 * math.log(2.0)), ALU.mult, ALU.add)
+        horner = tile("horner", TERMS + 4)
         nc.vector.tensor_tensor_scan(horner[:], horner_x, series[:], 0.0, ALU.mult, ALU.add)
 
         values_half(1, "sum_b")
@@ -167,14 +169,12 @@ def tile_attend_gpagreement_kernel(tc, query, query2, keys_words, keys_scales, g
         for half in (slice(0, I // 2), slice(I // 2, I)):
             nc.vector.tensor_tensor(diff[:, half], b_ps[:, half], neg_a[:, half], ALU.add)
         y = tile("y", I)
-        nc.scalar.activation(y[:], diff[:], ACT.Tanh, bias=horner[:, TERMS + 1 :], scale=0.5)
+        nc.scalar.activation(y[:], diff[:], ACT.Tanh, bias=horner[:, TERMS + 3 :], scale=0.5)
         r2 = tile("r2", I)
         nc.scalar.activation(r2[:], y[:], ACT.Square, bias=0.5, scale=0.5)
 
-        factor = tile("factor", 1)
-        nc.vector.tensor_scalar_mul(factor[:], row_factor[:], PENALTY)
         wac = tile("wac", I)
-        nc.scalar.activation(wac[:], wa[:], ACT.Copy, scale=factor[:])
+        nc.scalar.activation(wac[:], wa[:], ACT.Copy, scale=row_factor[:])
 
         nc.vector.tensor_tensor(
             ws[:].rearrange("p (s j) -> p s j", j=PACK),
@@ -187,9 +187,9 @@ def tile_attend_gpagreement_kernel(tc, query, query2, keys_words, keys_scales, g
 
         wd = tile("wd", I)
         m = tile("m", 1)
-        nc.vector.scalar_tensor_tensor(wd[:], r2[:], 1.0, wv[:], ALU.mult, ALU.mult, accum_out=m[:])
+        nc.vector.scalar_tensor_tensor(wd[:], r2[:], math.sqrt(PENALTY), wv[:], ALU.mult, ALU.mult, accum_out=m[:])
         wdy = tile("wdy", I)
-        nc.vector.scalar_tensor_tensor(wdy[:], y[:], factor[:], wd[:], ALU.mult, ALU.mult)
+        nc.vector.scalar_tensor_tensor(wdy[:], y[:], row_factor[:], wd[:], ALU.mult, ALU.mult)
         neg_da = tile("neg_da", I)
         nc.vector.scalar_tensor_tensor(neg_da[:], wa[:], m[:], wd[:], ALU.mult, ALU.subtract)
         neg_wz = tile("neg_wz", I)

@@ -23,6 +23,8 @@ PACK = 4
 TERMS = 20
 EXPONENT_BITS = 0x7F800000
 PENALTY = 512.0 * 2.0 * 512.0
+VECTOR_CLEARS = 768
+HALVES = (slice(0, I // 2), slice(I // 2, I))
 STORE_EDGES = (0, 256, 768, 1280, 1792, 2048)
 
 
@@ -52,9 +54,9 @@ def tile_attend_gpagreement_kernel(tc, query, query2, keys_words, keys_scales, g
             nc.sync.dma_start(raw[:], src.rearrange("(p j) w -> p j w", j=PACK))
             return raw
 
-        nc.sync.dma_start(offsets[:], offs)
         k_words = tile("k_words", T, U16)
         nc.sync.dma_start(k_words[:].bitcast(I32), keys_words[0].bitcast(I32))
+        nc.sync.dma_start(offsets[:], offs)
         load_scales(k_scales, keys_scales)
         q1_raw = load_rows("q1_raw", query)
         q2_raw = load_rows("q2_raw", query2)
@@ -87,7 +89,8 @@ def tile_attend_gpagreement_kernel(tc, query, query2, keys_words, keys_scales, g
         horner_x = ws[:, : TERMS + 4]
         for col, value in ((TERMS + 1, 1.0), (TERMS + 2, -1.0), (TERMS + 3, -0.5)):
             nc.vector.memset(horner_x[:, col : col + 1], value)
-        nc.vector.memset(window[:], 0.0)
+        nc.vector.memset(window[:, :VECTOR_CLEARS], 0.0)
+        nc.gpsimd.memset(window[:, VECTOR_CLEARS:], 0.0)
 
         def interleave(name, raw):
             grouped = sb.tile([P, Q, PACK], BF16, name=name, align_bytes=64)
@@ -153,7 +156,7 @@ def tile_attend_gpagreement_kernel(tc, query, query2, keys_words, keys_scales, g
             cols = slice(h * I // 2, (h + 1) * I // 2)
             nc.tensor.matmul_mx(c_ps[:, cols], lhsT=go_mx[0][:].bitcast(FP8X4), lhsT_scale=go_mx[1][:], rhs=picked[:].bitcast(FP4X4), rhs_scale=vg_scales[:, cols], start=True, stop=True)
 
-        values_half(0, "go_bf")
+        values_half(0, None)
 
         neg_ratio = tile("neg_ratio", 1)
         nc.vector.tensor_scalar(neg_ratio[:], sum_b[:], inv_sum_a[:], -1.0, ALU.mult, ALU.mult)
@@ -161,17 +164,19 @@ def tile_attend_gpagreement_kernel(tc, query, query2, keys_words, keys_scales, g
         nc.vector.tensor_scalar(pow2[:], neg_ratio[:].bitcast(I32), EXPONENT_BITS, EXPONENT_BITS, ALU.bitwise_and, ALU.bitwise_xor)
         nc.vector.tensor_scalar(horner_x[:, : TERMS + 1], neg_ratio[:].to_broadcast([P, TERMS + 1]), pow2[:].bitcast(F32), 3.0, ALU.mult, ALU.add)
         nc.vector.tensor_scalar(series[:, TERMS : TERMS + 1], pow2[:], math.log(2.0) / 2.0**23, -(math.log(3.0) + 127.0 * math.log(2.0)), ALU.mult, ALU.add)
+        values_half(1, "neg_ratio")
         horner = tile("horner", TERMS + 4)
         nc.vector.tensor_tensor_scan(horner[:], horner_x, series[:], 0.0, ALU.mult, ALU.add)
 
-        values_half(1, "sum_b")
         diff = tile("diff", I, tag="pb")
-        for half in (slice(0, I // 2), slice(I // 2, I)):
+        for half in HALVES:
             nc.vector.tensor_tensor(diff[:, half], b_ps[:, half], neg_a[:, half], ALU.add)
         y = tile("y", I)
-        nc.scalar.activation(y[:], diff[:], ACT.Tanh, bias=horner[:, TERMS + 3 :], scale=0.5)
         r2 = tile("r2", I)
-        nc.scalar.activation(r2[:], y[:], ACT.Square, bias=0.5, scale=0.5)
+        for half in HALVES:
+            nc.scalar.activation(y[:, half], diff[:, half], ACT.Tanh, bias=horner[:, TERMS + 3 :], scale=0.5)
+        for half in HALVES:
+            nc.scalar.activation(r2[:, half], y[:, half], ACT.Square, bias=0.5, scale=0.5)
 
         wac = tile("wac", I)
         nc.scalar.activation(wac[:], wa[:], ACT.Copy, scale=row_factor[:])
@@ -183,13 +188,18 @@ def tile_attend_gpagreement_kernel(tc, query, query2, keys_words, keys_scales, g
             ALU.mult,
         )
         wv = tile("wv", I)
-        nc.vector.tensor_tensor(wv[:], c_ps[:], ws[:], ALU.mult)
+        for half in HALVES:
+            nc.vector.tensor_tensor(wv[:, half], c_ps[:, half], ws[:, half], ALU.mult)
 
         wd = tile("wd", I)
         m = tile("m", 1)
-        nc.vector.scalar_tensor_tensor(wd[:], r2[:], math.sqrt(PENALTY), wv[:], ALU.mult, ALU.mult, accum_out=m[:])
+        m_parts = tile("m_parts", 2)
+        for h, half in enumerate(HALVES):
+            nc.vector.scalar_tensor_tensor(wd[:, half], r2[:, half], math.sqrt(PENALTY), wv[:, half], ALU.mult, ALU.mult, accum_out=m_parts[:, h : h + 1])
         wdy = tile("wdy", I)
-        nc.vector.scalar_tensor_tensor(wdy[:], y[:], row_factor[:], wd[:], ALU.mult, ALU.mult)
+        nc.vector.scalar_tensor_tensor(wdy[:, HALVES[0]], y[:, HALVES[0]], row_factor[:], wd[:, HALVES[0]], ALU.mult, ALU.mult)
+        nc.vector.tensor_tensor(m[:], m_parts[:, 0:1], m_parts[:, 1:2], ALU.add)
+        nc.vector.scalar_tensor_tensor(wdy[:, HALVES[1]], y[:, HALVES[1]], row_factor[:], wd[:, HALVES[1]], ALU.mult, ALU.mult)
         neg_da = tile("neg_da", I)
         nc.vector.scalar_tensor_tensor(neg_da[:], wa[:], m[:], wd[:], ALU.mult, ALU.subtract)
         neg_wz = tile("neg_wz", I)

import math
from contextlib import ExitStack

import concourse.mybir as mybir
from concourse.masks import make_identity

D, E, T, I, Q = 512, 512, 2048, 512, 128
FLOPS = 3 * 2 * D * Q * I

F32 = mybir.dt.float32
BF16 = mybir.dt.bfloat16
I32 = mybir.dt.int32
U32 = mybir.dt.uint32
U16 = mybir.dt.uint16
U8 = mybir.dt.uint8
FP8X4 = mybir.dt.float8_e4m3fn_x4
FP4X4 = mybir.dt.float4_e2m1fn_x4
ALU = mybir.AluOpType
ACT = mybir.ActivationFunctionType

P = 128
PACK = 4
TERMS = 20
EXPONENT_BITS = 0x7F800000
PENALTY = 512.0 * 2.0 * 512.0
VECTOR_CLEARS = 768
HALVES = (slice(0, I // 2), slice(I // 2, I))
STORE_EDGES = (0, 256, 768, 1280, 1792, 2048)


def tile_attend_gpagreement_kernel(tc, query, query2, keys_words, keys_scales, gout, vals_words, vals_scales, size, base, gq1, offs, out):
    nc = tc.nc
    with ExitStack() as ctx:
        sb = ctx.enter_context(tc.tile_pool(name="sb", bufs=1))
        ps = ctx.enter_context(tc.psum_pool(name="ps", bufs=1))

        def tile(name, cols, dtype=F32, tag=None):
            return sb.tile([P, cols], dtype, name=name, tag=tag or name, align_bytes=64)

        offsets = sb.tile([P, I // 16], U16, name="offsets")
        k_scales = tile("k_scales", T, U8)
        v_scales = tile("v_scales", T, U8)
        window = tile("window", T)

        nc.vector.memset(k_scales[:].bitcast(I32), 0)
        nc.vector.memset(v_scales[:].bitcast(I32), 0)

        def load_scales(dst, src):
            for r in range(4):
                nc.sync.dma_start(dst[r:P:32, :].bitcast(I32), src[0, r:16:4, :].bitcast(I32))

        def load_rows(name, src, tag=None):
            raw = sb.tile([P, PACK, Q], F32, name=name, tag=tag or name, align_bytes=64)
            nc.sync.dma_start(raw[:], src.rearrange("(p j) w -> p j w", j=PACK))
            return raw

        k_words = tile("k_words", T, U16)
        nc.sync.dma_start(k_words[:].bitcast(I32), keys_words[0].bitcast(I32))
        nc.sync.dma_start(offsets[:], offs)
        load_scales(k_scales, keys_scales)
        q1_raw = load_rows("q1_raw", query)
        q2_raw = load_rows("q2_raw", query2)
        load_scales(v_scales, vals_scales)
        go_raw = load_rows("go_raw", gout)
        v_words = tile("v_words", T, U16)
        nc.sync.dma_start(v_words[:].bitcast(I32), vals_words[0].bitcast(I32))
        size_col = tile("size_col", PACK)
        nc.sync.dma_start(size_col[:], size.rearrange("o (p j) -> (o p) j", j=PACK))
        row_factor = tile("row_factor", 1)
        nc.sync.dma_start(row_factor[:], gq1)
        base_sb = tile("base_sb", T)
        nc.sync.dma_start(base_sb[:], base)

        order = tile("order", TERMS)
        nc.gpsimd.iota(order[:], pattern=[[-1, TERMS]], base=TERMS, channel_multiplier=0, allow_small_or_imprecise_dtypes=True)
        ident = tile("ident", P)
        make_identity(nc, ident[:])

        powers = tile("powers", TERMS)
        nc.scalar.activation(powers[:], order[:], ACT.Exp, scale=-math.log(3.0))
        inv_order = tile("inv_order", TERMS)
        nc.vector.reciprocal(inv_order[:], order[:])
        series = tile("series", TERMS + 4)
        nc.vector.tensor_tensor(series[:, :TERMS], powers[:], inv_order[:], ALU.mult)
        nc.vector.memset(series[:, TERMS + 3 :], 0.0)
        neg_max_b = series[:, TERMS + 1 : TERMS + 2]
        neg_max_a = series[:, TERMS + 2 : TERMS + 3]
        ws = tile("ws", I)
        horner_x = ws[:, : TERMS + 4]
        for col, value in ((TERMS + 1, 1.0), (TERMS + 2, -1.0), (TERMS + 3, -0.5)):
            nc.vector.memset(horner_x[:, col : col + 1], value)
        nc.vector.memset(window[:, :VECTOR_CLEARS], 0.0)
        nc.gpsimd.memset(window[:, VECTOR_CLEARS:], 0.0)

        def interleave(name, raw):
            grouped = sb.tile([P, Q, PACK], BF16, name=name, align_bytes=64)
            nc.scalar.copy(grouped[:], raw[:].rearrange("p j w -> p w j"))
            return grouped

        def quantize(name, grouped, tag=None):
            codes = tile(name + "_codes", Q, U32, tag=tag)
            scales = tile(name + "_scales", Q, U8)
            nc.vector.quantize_mx(codes[:].bitcast(FP8X4), scales[:], grouped[:].rearrange("p w j -> p (w j)"))
            return codes, scales

        def gather(name, pool_tile, dtype, tag=None):
            picked = tile(name, I, dtype, tag=tag)
            nc.vector.tensor_copy(picked[:], pool_tile[:].indirect(offsets[:]))
            return picked

        def product(name, rows, words, scales):
            acc = ps.tile([P, I], F32, name=name)
            nc.tensor.matmul_mx(acc[:], lhsT=rows[0][:].bitcast(FP8X4), lhsT_scale=rows[1][:], rhs=words[:].bitcast(FP4X4), rhs_scale=scales[:], start=True, stop=True)
            return acc

        q1_bf = interleave("q1_bf", q1_raw)
        q2_bf = interleave("q2_bf", q2_raw)
        go_bf = interleave("go_bf", go_raw)

        kg_words = gather("kg_words", k_words, U16)
        kg_scales = gather("kg_scales", k_scales, U8)
        q1_mx = quantize("q1", q1_bf)
        a_ps = product("a_ps", q1_mx, kg_words, kg_scales)
        q2_mx = quantize("q2", q2_bf)
        b_ps = product("b_ps", q2_mx, kg_words, kg_scales)
        vg_scales = gather("vg_scales", v_scales, U8)

        size_ps = ps.tile([P, PACK, P], F32, name="size_ps")
        for j in range(PACK):
            nc.tensor.transpose(size_ps[:, j, :], size_col[:, j : j + 1].to_broadcast([P, P]), ident[:])

        neg_scores = tile("neg_scores", 2 * I, tag="v_scales")
        neg_a = neg_scores[:, :I]
        neg_b = neg_scores[:, I:]
        nc.vector.tensor_scalar(neg_a[:], a_ps[:], -1.0, None, ALU.mult, ALU.min, accum_out=neg_max_a[:])
        nc.vector.tensor_scalar(neg_b[:], b_ps[:], -1.0, None, ALU.mult, ALU.min, accum_out=neg_max_b[:])

        pa = tile("pa", I, tag="go_raw")
        sum_a = tile("sum_a", 1)
        nc.scalar.activation(pa[:], a_ps[:], ACT.Exp, bias=neg_max_a[:], accum_out=sum_a[:])
        pb = tile("pb", I)
        sum_b = tile("sum_b", 1)
        nc.scalar.activation(pb[:], b_ps[:], ACT.Exp, bias=neg_max_b[:], accum_out=sum_b[:])

        inv_sum_a = tile("inv_sum_a", 1)
        nc.vector.reciprocal(inv_sum_a[:], sum_a[:])
        wa = tile("wa", I)
        nc.scalar.activation(wa[:], pa[:], ACT.Copy, scale=inv_sum_a[:])

        go_mx = quantize("go", go_bf, tag="q2_codes")
        c_ps = ps.tile([P, I], F32, name="c_ps")

        def values_half(h, tag):
            picked = tile("vg_words%d" % h, I // 2, U16, tag=tag)
            nc.vector.tensor_copy(picked[:], v_words[:].indirect(offsets[:, h * I // 32 : (h + 1) * I // 32]))
            cols = slice(h * I // 2, (h + 1) * I // 2)
            nc.tensor.matmul_mx(c_ps[:, cols], lhsT=go_mx[0][:].bitcast(FP8X4), lhsT_scale=go_mx[1][:], rhs=picked[:].bitcast(FP4X4), rhs_scale=vg_scales[:, cols], start=True, stop=True)

        values_half(0, None)

        neg_ratio = tile("neg_ratio", 1)
        nc.vector.tensor_scalar(neg_ratio[:], sum_b[:], inv_sum_a[:], -1.0, ALU.mult, ALU.mult)
        pow2 = tile("pow2", 1, I32)
        nc.vector.tensor_scalar(pow2[:], neg_ratio[:].bitcast(I32), EXPONENT_BITS, EXPONENT_BITS, ALU.bitwise_and, ALU.bitwise_xor)
        nc.vector.tensor_scalar(horner_x[:, : TERMS + 1], neg_ratio[:].to_broadcast([P, TERMS + 1]), pow2[:].bitcast(F32), 3.0, ALU.mult, ALU.add)
        nc.vector.tensor_scalar(series[:, TERMS : TERMS + 1], pow2[:], math.log(2.0) / 2.0**23, -(math.log(3.0) + 127.0 * math.log(2.0)), ALU.mult, ALU.add)
        values_half(1, "neg_ratio")
        horner = tile("horner", TERMS + 4)
        nc.vector.tensor_tensor_scan(horner[:], horner_x, series[:], 0.0, ALU.mult, ALU.add)

        diff = tile("diff", I, tag="pb")
        for half in HALVES:
            nc.vector.tensor_tensor(diff[:, half], b_ps[:, half], neg_a[:, half], ALU.add)
        y = tile("y", I)
        r2 = tile("r2", I)
        for half in HALVES:
            nc.scalar.activation(y[:, half], diff[:, half], ACT.Tanh, bias=horner[:, TERMS + 3 :], scale=0.5)
        for half in HALVES:
            nc.scalar.activation(r2[:, half], y[:, half], ACT.Square, bias=0.5, scale=0.5)

        wac = tile("wac", I)
        nc.scalar.activation(wac[:], wa[:], ACT.Copy, scale=row_factor[:])

        nc.vector.tensor_tensor(
            ws[:].rearrange("p (s j) -> p s j", j=PACK),
            size_ps[:].rearrange("p j s -> p s j"),
            wa[:].rearrange("p (s j) -> p s j", j=PACK),
            ALU.mult,
        )
        wv = tile("wv", I)
        for half in HALVES:
            nc.vector.tensor_tensor(wv[:, half], c_ps[:, half], ws[:, half], ALU.mult)

        wd = tile("wd", I)
        m = tile("m", 1)
        m_parts = tile("m_parts", 2)
        for h, half in enumerate(HALVES):
            nc.vector.scalar_tensor_tensor(wd[:, half], r2[:, half], math.sqrt(PENALTY), wv[:, half], ALU.mult, ALU.mult, accum_out=m_parts[:, h : h + 1])
        wdy = tile("wdy", I)
        nc.vector.scalar_tensor_tensor(wdy[:, HALVES[0]], y[:, HALVES[0]], row_factor[:], wd[:, HALVES[0]], ALU.mult, ALU.mult)
        nc.vector.tensor_tensor(m[:], m_parts[:, 0:1], m_parts[:, 1:2], ALU.add)
        nc.vector.scalar_tensor_tensor(wdy[:, HALVES[1]], y[:, HALVES[1]], row_factor[:], wd[:, HALVES[1]], ALU.mult, ALU.mult)
        neg_da = tile("neg_da", I)
        nc.vector.scalar_tensor_tensor(neg_da[:], wa[:], m[:], wd[:], ALU.mult, ALU.subtract)
        neg_wz = tile("neg_wz", I)
        nc.vector.scalar_tensor_tensor(neg_wz[:], wac[:], m[:], wdy[:], ALU.mult, ALU.subtract)
        neg_n = tile("neg_n", 1)
        wada = tile("wada", I)
        nc.vector.scalar_tensor_tensor(wada[:], neg_da[:], 1.0, wa[:], ALU.mult, ALU.mult, accum_out=neg_n[:])
        wt = tile("wt", I)
        total = tile("total", 1)
        nc.vector.scalar_tensor_tensor(wt[:], neg_da[:], neg_n[:], neg_wz[:], ALU.subtract, ALU.mult, accum_out=total[:])
        tw = tile("tw", I)
        nc.vector.tensor_scalar(tw[:], wa[:], total[:], -1.0, ALU.mult, ALU.mult)
        nc.vector.tensor_tensor(window[:].indirect(offsets[:]), wt[:], tw[:], ALU.add)

        for n in range(len(STORE_EDGES) - 1):
            cols = slice(STORE_EDGES[n], STORE_EDGES[n + 1])
            nc.vector.tensor_tensor(base_sb[:, cols], base_sb[:, cols], window[:, cols], ALU.add)
            queue = nc.sync if n % 2 == 0 else nc.scalar
            queue.dma_start(out[:, cols], base_sb[:, cols])
